import numpy as np
import ml_dtypes


def mxq(x, axis, fmt="e4m3"):
    dtype, down = {"e4m3": (ml_dtypes.float8_e4m3fn, 7), "e5m2": (ml_dtypes.float8_e5m2, 14)}[fmt]
    v = np.moveaxis(np.asarray(x, np.float32).astype(ml_dtypes.bfloat16).astype(np.float64), axis, -1)
    blocks = v.reshape(v.shape[:-1] + (-1, 32))
    amax = np.abs(blocks).max(-1, keepdims=True)
    byte = np.maximum(np.where(amax > 0, np.frexp(amax)[1] - 1 + 127, 0) - down, 1)
    scale = np.exp2(byte - 127.0)
    codes = (blocks / scale).astype(np.float32).astype(dtype).astype(np.float64)
    return np.moveaxis((codes * scale).reshape(v.shape), -1, axis)


WIDE = False


def mx_kscale(k):
    if not WIDE:
        return np.ones(k)
    levels = np.array([10, -10, 5, -5, 0])
    if k % 512:
        return np.exp2(np.random.permutation(np.resize(levels, k // 32))).repeat(32)
    a = np.empty((k // 512, 16))
    for p in range(k // 512):
        a[p, :8] = np.random.permutation(np.resize(levels, 8))
        for g in range(8):
            far = levels[np.abs(levels - a[p, g]) >= 10]
            a[p, g + 8] = far[np.random.randint(len(far))]
    return np.exp2(a.ravel()).repeat(32)


def f64(x):
    return np.asarray(x).astype(np.float64)


def striped(idx):
    return np.tile(idx.reshape(-1, 16).T, (8, 1)).astype(np.uint16)


def unstriped(offs):
    return offs[:16].T.reshape(-1).astype(np.int64)


def pack_weight(w):
    k, n = w.shape
    w = f64(np.asarray(w, np.float32).astype(ml_dtypes.bfloat16)).reshape(k // 32, 32, n)
    amax = np.abs(w).max(1)
    byte = np.clip(np.where(amax > 0, np.frexp(amax)[1] - 1 + 127 - 7, 1), 1, 254)
    scaled = (w * np.exp2(127.0 - byte)[:, None, :]).reshape(k, n).astype(np.float32)
    words = np.ascontiguousarray(scaled.reshape(k // 512, 128, 4, n).transpose(0, 1, 3, 2)).astype(ml_dtypes.float8_e4m3fn).view(np.uint8)
    return words, np.ascontiguousarray(byte.astype(np.uint8).reshape(k // 512, 16, n))


def unpack_weight(words, scales):
    g, p, n, _ = words.shape
    vals = np.ascontiguousarray(words).view(ml_dtypes.float8_e4m3fn).astype(np.float64) * np.repeat(np.exp2(scales.astype(np.float64) - 127.0), 8, axis=1)[..., None]
    return vals.transpose(0, 1, 3, 2).reshape(g * 512, n)


E2M1 = np.array([0.0, 0.5, 1.0, 1.5, 2.0, 3.0, 4.0, 6.0, -0.0, -0.5, -1.0, -1.5, -2.0, -3.0, -4.0, -6.0])


def pack_fp4(w):
    k, n = w.shape
    w = f64(np.asarray(w, np.float32).astype(ml_dtypes.bfloat16)).reshape(k // 32, 32, n)
    amax = np.abs(w).max(1)
    mant, ex = np.frexp(amax / 6.0)
    byte = np.clip(np.where(amax > 0, np.where(mant > 0.5, ex, ex - 1) + 127, 1), 1, 254)
    scaled = (w * np.exp2(127.0 - byte)[:, None, :]).reshape(k, n).astype(np.float32)
    c = np.ascontiguousarray(scaled.reshape(k // 512, 128, 4, n).transpose(0, 1, 3, 2)).astype(ml_dtypes.float4_e2m1fn).view(np.uint8) & 0xF
    words = (c[..., 0::2] | (c[..., 1::2] << 4)).reshape(k // 512, 128, 2 * n)
    return np.ascontiguousarray(words), np.ascontiguousarray(byte.astype(np.uint8).reshape(k // 512, 16, n))


def unpack_fp4(words, scales):
    g, _, n = scales.shape
    words = np.ascontiguousarray(words).reshape(g, 128, n, 2)
    nib = np.empty((g, 128, n, 4), np.uint8)
    nib[..., 0::2] = words & 0xF
    nib[..., 1::2] = words >> 4
    vals = E2M1[nib] * np.repeat(np.exp2(scales.astype(np.float64) - 127.0), 8, axis=1)[..., None]
    return vals.transpose(0, 1, 3, 2).reshape(g * 512, n)


def planes(y):
    n, m = y.shape
    v = y.astype(np.float32).astype(ml_dtypes.bfloat16).astype(np.float64).reshape(n // 32, 32, m)
    top = np.abs(v).max(1)
    byte = np.clip(np.where(top > 0, np.frexp(top)[1] - 1 + 127 - 7, 1), 1, 254)
    codes = (v * np.exp2(127.0 - byte)[:, None, :]).reshape(n, m).astype(np.float32).astype(ml_dtypes.float8_e4m3fn).view(np.uint8)
    words = codes.reshape(n // 512, 128, 4, m).transpose(0, 1, 3, 2)
    return np.ascontiguousarray(words), np.ascontiguousarray(byte.astype(np.uint8).reshape(n // 512, 16, m))


K, T, S, N, H, U = 512, 2048, 512, 512, 512, 1024


def setup_inputs():
    n = np.random.standard_normal
    s = mx_kscale(K)[:, None]
    u = mx_kscale(H)
    packed_xT = pack_weight(n((K, T)) * s)
    packed_w1 = pack_fp4(n((K, N)) / np.sqrt(K) / s)
    packed_w2 = pack_fp4(n((K, N)) / np.sqrt(K) / s)
    packed_w3 = pack_fp4(n((H, N)) / np.sqrt(H) / u[:, None])
    return {
        "x_words": packed_xT[0],
        "x_scales": packed_xT[1],
        "w1_words": packed_w1[0],
        "w1_scales": packed_w1[1],
        "w2_words": packed_w2[0],
        "w2_scales": packed_w2[1],
        "unit": (np.random.uniform(0.6, 1.4, (H, 1)) * u[:, None]).astype(np.float32),
        "w3_words": packed_w3[0],
        "w3_scales": packed_w3[1],
        "offs": striped(np.random.permutation(T)[:S]),
        "pk": striped(np.random.permutation(np.concatenate([np.arange(S), np.random.randint(0, S, U - S)]))),
        "dp1": striped(np.random.permutation(np.concatenate([np.arange(S), np.random.randint(0, S, U - S)]))),
        "dp2": striped(np.random.permutation(np.concatenate([np.arange(S), np.random.randint(0, S, U - S)]))),
    }


def reference(x_words, x_scales, w1_words, w1_scales, w2_words, w2_scales, unit, w3_words, w3_scales, offs, pk, dp1, dp2):
    xq = unpack_weight(x_words, x_scales)[:, unstriped(offs)]
    y = unpack_fp4(w1_words, w1_scales).T @ xq
    y_1 = y[:, unstriped(dp1)]
    y_2 = y[:, unstriped(dp2)]
    cmp1 = y_1 * y_2
    z1 = unpack_fp4(w2_words, w2_scales).T @ xq
    zp = z1[:, unstriped(pk)]
    cfl = cmp1 - zp
    z_1 = z1[:, unstriped(dp1)]
    hid = f64(unit) * (cfl * z_1)
    out_0 = unpack_fp4(w3_words, w3_scales).T @ mxq(hid, 0, "e4m3")
    return (out_0,) + planes(out_0)

@@ -1,0 +1,200 @@
+from contextlib import ExitStack
+
+import concourse.mybir as mybir
+
+F32 = mybir.dt.float32
+BF16 = mybir.dt.bfloat16
+I32 = mybir.dt.int32
+U32 = mybir.dt.uint32
+U16 = mybir.dt.uint16
+U8 = mybir.dt.uint8
+FP8X4 = mybir.dt.float8_e4m3fn_x4
+FP4X4 = mybir.dt.float4_e2m1fn_x4
+MULT = mybir.AluOpType.mult
+ADD = mybir.AluOpType.add
+COPY = mybir.ActivationFunctionType.Copy
+
+P = 128
+PACK = 4
+T, S, U = 2048, 512, 1024
+FLOPS = 2 * 512 * 512 * (S + S + U)
+CHUNKS = (256, 384, 256, 128)
+SUB = 128
+
+
+def load_scale_rows(queues, plane, rows):
+    for q in range(4):
+        queues[q].dma_start(
+            out=plane[32 * q : 32 * q + 4, :].bitcast(I32),
+            in_=rows[0, 4 * q : 4 * q + 4, :].bitcast(I32),
+        )
+
+
+def deal_words(nc, raw_words, words):
+    nc.vector.tensor_copy(
+        out=words[:].rearrange("p (t m b) -> p t m b", t=PACK, b=2),
+        in_=raw_words[:].rearrange("p (m t b) -> p t m b", t=PACK, b=2),
+    )
+
+
+def deal_scales(nc, raw_scales, scales):
+    nc.vector.tensor_copy(
+        out=scales[:].rearrange("p (t m) -> p t m", t=PACK),
+        in_=raw_scales[:].rearrange("p (m t) -> p t m", t=PACK),
+    )
+
+
+def tile_picked_yresolv_cfl_po_kernel(
+    tc, x_words, x_scales, w1_words, w1_scales, w2_words, w2_scales, unit,
+    w3_words, w3_scales, offs, pk, dp1, dp2, out_0, out_1, out_2,
+):
+    nc = tc.nc
+    with ExitStack() as ctx:
+        keep = ctx.enter_context(tc.tile_pool(name="keep", bufs=1))
+        first = ctx.enter_context(tc.psum_pool(name="first", bufs=4))
+        last = ctx.enter_context(tc.psum_pool(name="last", bufs=4))
+
+        offs_sb = keep.tile([P, S // 16], U16, name="offs_sb")
+        pk_sb = keep.tile([P, U // 16], U16, name="pk_sb")
+        dp1_sb = keep.tile([P, U // 16], U16, name="dp1_sb")
+        dp2_sb = keep.tile([P, U // 16], U16, name="dp2_sb")
+        table_words = keep.tile([P, T], U32, name="table_words", align_bytes=64)
+        table_scales = keep.tile([P, T], U8, name="table_scales", align_bytes=64)
+        raw_words = [keep.tile([P, 2 * S], U8, name="raw_words%d" % i) for i in range(2)]
+        raw_scales = [keep.tile([P, S], U8, name="raw_scales%d" % i) for i in range(2)]
+        w_words = [keep.tile([P, 2 * S], U8, name="w_words%d" % i, align_bytes=64) for i in range(3)]
+        w_scales = [keep.tile([P, S], U8, name="w_scales%d" % i, align_bytes=64) for i in range(3)]
+        unit_sb = keep.tile([P, PACK], F32, name="unit_sb")
+
+        nc.vector.memset(table_scales[:].bitcast(I32), 0)
+        for i in range(2):
+            nc.vector.memset(raw_scales[i][:].bitcast(I32), 0)
+
+        nc.sync.dma_start(offs_sb[:], offs)
+        nc.sync.dma_start(out=raw_words[0][:].bitcast(I32), in_=w1_words[0].bitcast(I32))
+        nc.sync.dma_start(
+            out=table_words[:].bitcast(I32),
+            in_=x_words[0].rearrange("p n t -> p (n t)").bitcast(I32),
+        )
+        load_scale_rows([nc.scalar] * 4, table_scales, x_scales)
+        load_scale_rows([nc.scalar] * 3 + [nc.gpsimd], raw_scales[0], w1_scales)
+        nc.sync.dma_start(dp1_sb[:], dp1)
+        nc.sync.dma_start(out=raw_words[1][:].bitcast(I32), in_=w2_words[0].bitcast(I32))
+        load_scale_rows([nc.sync] * 4, raw_scales[1], w2_scales)
+        nc.sync.dma_start(dp2_sb[:], dp2)
+        nc.sync.dma_start(out=unit_sb[:], in_=unit.rearrange("(p t) o -> p (t o)", t=PACK))
+        nc.sync.dma_start(pk_sb[:], pk)
+
+        x_codes = keep.tile([P, S], U32, name="x_codes", align_bytes=64)
+        x_plane = keep.tile([P, S], U8, name="x_plane", align_bytes=64)
+        deal_words(nc, raw_words[0], w_words[0])
+        nc.vector.tensor_copy(x_plane[:], table_scales[:].indirect(offs_sb[:]))
+        nc.vector.tensor_copy(x_codes[:], table_words[:].indirect(offs_sb[:]))
+        deal_scales(nc, raw_scales[0], w_scales[0])
+        deal_words(nc, raw_words[1], w_words[1])
+        deal_scales(nc, raw_scales[1], w_scales[1])
+        nc.sync.dma_start(out=raw_words[0][:].bitcast(I32), in_=w3_words[0].bitcast(I32))
+        load_scale_rows([nc.sync] * 4, raw_scales[0], w3_scales)
+
+        def stationary(i, t):
+            return (
+                w_words[i][:, 2 * P * t : 2 * P * (t + 1)].bitcast(FP4X4),
+                w_scales[i][:, P * t : P * (t + 1)],
+            )
+
+        y = [keep.tile([P, S], F32, name="y%d" % t) for t in range(PACK)]
+        z_neg = [keep.tile([P, S], F32, name="z_neg%d" % t) for t in range(PACK)]
+        z_unit = [keep.tile([P, S], F32, name="z_unit%d" % t) for t in range(PACK)]
+
+        def project(t):
+            banks = []
+            for i in range(2):
+                bank = first.tile([P, S], F32, name="bank")
+                words, scales = stationary(i, t)
+                nc.tensor.matmul_mx(
+                    out=bank[:], lhsT=words, lhsT_scale=scales,
+                    rhs=x_codes[:].bitcast(FP8X4), rhs_scale=x_plane[:],
+                    start=True, stop=True,
+                )
+                banks.append(bank)
+            nc.scalar.activation(y[t][:], banks[0][:], COPY)
+            nc.vector.tensor_scalar_mul(z_neg[t][:], banks[1][:], -1.0)
+            nc.vector.tensor_scalar(
+                z_unit[t][:], z_neg[t][:], unit_sb[:, t : t + 1], -1.0, MULT, MULT
+            )
+
+        out_codes = keep.tile([P, U], U32, name="out_codes", align_bytes=64)
+        out_plane = keep.tile([P, U], U8, name="out_plane", align_bytes=64)
+        out_rows = out_0.rearrange("(p t) r -> p t r", t=PACK)
+        out_words = out_1[0].rearrange("p n t -> p (n t)")
+
+        r0 = 0
+        for c, n in enumerate(CHUNKS):
+            cols = slice(r0 // 16, (r0 + n) // 16)
+            cfl = keep.tile([P, PACK, n], F32, name="cfl%d" % c)
+            z_1 = keep.tile([P, PACK, n], F32, name="z_1_%d" % c)
+            cmp1 = []
+            for t in range(PACK + 1):
+                if t < PACK:
+                    if c == 0:
+                        project(t)
+                    y_1 = keep.tile([P, n], F32, name="y_1_%d_%d" % (c, t))
+                    prod = keep.tile([P, n], F32, name="cmp1_%d_%d" % (c, t))
+                    nc.scalar.activation(y_1[:], y[t][:].indirect(dp1_sb[:, cols]), COPY)
+                    nc.vector.tensor_tensor(prod[:], y[t][:].indirect(dp2_sb[:, cols]), y_1[:], MULT)
+                    nc.scalar.activation(z_1[:, t, :], z_unit[t][:].indirect(dp1_sb[:, cols]), COPY)
+                    cmp1.append(prod)
+                if t > 0:
+                    nc.vector.tensor_tensor(
+                        cfl[:, t - 1, :], z_neg[t - 1][:].indirect(pk_sb[:, cols]), cmp1[t - 1][:], ADD
+                    )
+            if c == 0:
+                deal_words(nc, raw_words[0], w_words[2])
+                deal_scales(nc, raw_scales[0], w_scales[2])
+
+            hid = keep.tile([P, n * PACK], BF16, name="hid%d" % c, align_bytes=64)
+            nc.vector.tensor_tensor(
+                hid[:].rearrange("p (j i t) -> p j t i", i=2, t=PACK),
+                cfl[:].rearrange("p t (j i) -> p j t i", i=2),
+                z_1[:].rearrange("p t (j i) -> p j t i", i=2),
+                MULT,
+            )
+            hid_codes = keep.tile([P, n], U32, name="hid_codes%d" % c, align_bytes=64)
+            hid_plane = keep.tile([P, n], U8, name="hid_plane%d" % c, align_bytes=64)
+            nc.vector.quantize_mx(out=hid_codes[:].bitcast(FP8X4), scales=hid_plane[:], in_=hid[:])
+
+            result = keep.tile([P, PACK, n], F32, name="result%d" % c)
+            rounded = keep.tile([P, n * PACK], BF16, name="rounded%d" % c, align_bytes=64)
+            for s0 in range(0, n, SUB):
+                acc = last.tile([P, PACK, SUB], F32, name="acc")
+                for t in range(PACK):
+                    words, scales = stationary(2, t)
+                    nc.tensor.matmul_mx(
+                        out=acc[:, t, :], lhsT=words, lhsT_scale=scales,
+                        rhs=hid_codes[:, s0 : s0 + SUB].bitcast(FP8X4),
+                        rhs_scale=hid_plane[:, s0 : s0 + SUB],
+                        start=True, stop=True,
+                    )
+                nc.scalar.copy(
+                    rounded[:, PACK * s0 : PACK * (s0 + SUB)].rearrange("p (j i t) -> p j t i", i=2, t=PACK),
+                    acc[:].rearrange("p t (j i) -> p j t i", i=2),
+                )
+                nc.scalar.copy(result[:, :, s0 : s0 + SUB], acc[:])
+            nc.vector.quantize_mx(
+                out=out_codes[:, r0 : r0 + n].bitcast(FP8X4),
+                scales=out_plane[:, r0 : r0 + n],
+                in_=rounded[:],
+            )
+            nc.sync.dma_start(out=out_rows[:, :, r0 : r0 + n], in_=result[:])
+            nc.sync.dma_start(
+                out=out_words[:, PACK * r0 : PACK * (r0 + n)].bitcast(I32),
+                in_=out_codes[:, r0 : r0 + n].bitcast(I32),
+            )
+            r0 = r0 + n
+
+        for q in range(4):
+            queue = nc.sync if q % 2 == 0 else nc.scalar
+            queue.dma_start(
+                out=out_2[0, 4 * q : 4 * q + 4, :].bitcast(I32),
+                in_=out_plane[32 * q : 32 * q + 4, :].bitcast(I32),
+            )

@@ -20,6 +20,8 @@ T, S, U = 2048, 512, 1024
 FLOPS = 2 * 512 * 512 * (S + S + U)
 CHUNKS = (256, 384, 256, 128)
 SUB = 128
+RING = 3
+ROUNDED_FROM_PSUM = 2
 
 
 def load_scale_rows(queues, plane, rows):
@@ -32,14 +34,14 @@ def load_scale_rows(queues, plane, rows):
 
 def deal_words(nc, raw_words, words):
     nc.vector.tensor_copy(
-        out=words[:].rearrange("p (t m b) -> p t m b", t=PACK, b=2),
+        out=words.rearrange("p (t m b) -> p t m b", t=PACK, b=2),
         in_=raw_words[:].rearrange("p (m t b) -> p t m b", t=PACK, b=2),
     )
 
 
 def deal_scales(nc, raw_scales, scales):
     nc.vector.tensor_copy(
-        out=scales[:].rearrange("p (t m) -> p t m", t=PACK),
+        out=scales.rearrange("p (t m) -> p t m", t=PACK),
         in_=raw_scales[:].rearrange("p (m t) -> p t m", t=PACK),
     )
 
@@ -58,42 +60,45 @@ def tile_picked_yresolv_cfl_po_kernel(
         pk_sb = keep.tile([P, U // 16], U16, name="pk_sb")
         dp1_sb = keep.tile([P, U // 16], U16, name="dp1_sb")
         dp2_sb = keep.tile([P, U // 16], U16, name="dp2_sb")
-        table_words = keep.tile([P, T], U32, name="table_words", align_bytes=64)
+        table_words = keep.tile([P, T], U32, name="table_words", tag="table", align_bytes=64)
         table_scales = keep.tile([P, T], U8, name="table_scales", align_bytes=64)
-        raw_words = [keep.tile([P, 2 * S], U8, name="raw_words%d" % i) for i in range(2)]
+        raw_words = [keep.tile([P, 2 * S], U8, name="raw_words%d" % i) for i in range(3)]
         raw_scales = [keep.tile([P, S], U8, name="raw_scales%d" % i) for i in range(2)]
         w_words = [keep.tile([P, 2 * S], U8, name="w_words%d" % i, align_bytes=64) for i in range(3)]
-        w_scales = [keep.tile([P, S], U8, name="w_scales%d" % i, align_bytes=64) for i in range(3)]
+        w3_plane = keep.tile([P, S], U8, name="w3_plane", align_bytes=64)
         unit_sb = keep.tile([P, PACK], F32, name="unit_sb")
 
         nc.vector.memset(table_scales[:].bitcast(I32), 0)
         for i in range(2):
             nc.vector.memset(raw_scales[i][:].bitcast(I32), 0)
 
-        nc.sync.dma_start(offs_sb[:], offs)
         nc.sync.dma_start(out=raw_words[0][:].bitcast(I32), in_=w1_words[0].bitcast(I32))
+        nc.sync.dma_start(offs_sb[:], offs)
+        load_scale_rows([nc.sync] * 4, table_scales, x_scales)
+        nc.sync.dma_start(out=raw_words[1][:].bitcast(I32), in_=w2_words[0].bitcast(I32))
         nc.sync.dma_start(
             out=table_words[:].bitcast(I32),
             in_=x_words[0].rearrange("p n t -> p (n t)").bitcast(I32),
         )
-        load_scale_rows([nc.scalar] * 4, table_scales, x_scales)
-        load_scale_rows([nc.scalar] * 3 + [nc.gpsimd], raw_scales[0], w1_scales)
+        load_scale_rows([nc.sync] * 4, raw_scales[0], w1_scales)
+        nc.gpsimd.dma_start(out=raw_words[2][:].bitcast(I32), in_=w3_words[0].bitcast(I32))
+        load_scale_rows([nc.gpsimd] + [nc.sync] * 3, raw_scales[1], w2_scales)
+        nc.gpsimd.dma_start(out=unit_sb[:], in_=unit.rearrange("(p t) o -> p (t o)", t=PACK))
         nc.sync.dma_start(dp1_sb[:], dp1)
-        nc.sync.dma_start(out=raw_words[1][:].bitcast(I32), in_=w2_words[0].bitcast(I32))
-        load_scale_rows([nc.sync] * 4, raw_scales[1], w2_scales)
         nc.sync.dma_start(dp2_sb[:], dp2)
-        nc.sync.dma_start(out=unit_sb[:], in_=unit.rearrange("(p t) o -> p (t o)", t=PACK))
         nc.sync.dma_start(pk_sb[:], pk)
 
         x_codes = keep.tile([P, S], U32, name="x_codes", align_bytes=64)
         x_plane = keep.tile([P, S], U8, name="x_plane", align_bytes=64)
-        deal_words(nc, raw_words[0], w_words[0])
+        deal_words(nc, raw_words[0], w_words[0][:])
         nc.vector.tensor_copy(x_plane[:], table_scales[:].indirect(offs_sb[:]))
+        deal_words(nc, raw_words[1], w_words[1][:])
+        deal_words(nc, raw_words[2], w_words[2][:])
         nc.vector.tensor_copy(x_codes[:], table_words[:].indirect(offs_sb[:]))
+        late = keep.tile([P, 2 * S], U8, name="late", tag="table", align_bytes=64)
+        w_scales = [late[:, 0:S], late[:, S : 2 * S], w3_plane[:]]
         deal_scales(nc, raw_scales[0], w_scales[0])
-        deal_words(nc, raw_words[1], w_words[1])
         deal_scales(nc, raw_scales[1], w_scales[1])
-        nc.sync.dma_start(out=raw_words[0][:].bitcast(I32), in_=w3_words[0].bitcast(I32))
         load_scale_rows([nc.sync] * 4, raw_scales[0], w3_scales)
 
         def stationary(i, t):
@@ -118,7 +123,7 @@ def tile_picked_yresolv_cfl_po_kernel(
                 )
                 banks.append(bank)
             nc.scalar.activation(y[t][:], banks[0][:], COPY)
-            nc.vector.tensor_scalar_mul(z_neg[t][:], banks[1][:], -1.0)
+            nc.scalar.mul(z_neg[t][:], banks[1][:], -1.0)
             nc.vector.tensor_scalar(
                 z_unit[t][:], z_neg[t][:], unit_sb[:, t : t + 1], -1.0, MULT, MULT
             )
@@ -128,43 +133,51 @@ def tile_picked_yresolv_cfl_po_kernel(
         out_rows = out_0.rearrange("(p t) r -> p t r", t=PACK)
         out_words = out_1[0].rearrange("p n t -> p (n t)")
 
-        r0 = 0
-        for c, n in enumerate(CHUNKS):
+        starts = [sum(CHUNKS[:c]) for c in range(len(CHUNKS))]
+        cfl, z_1, banks = {}, {}, {}
+        y_1_ring = [keep.tile([P, max(CHUNKS)], F32, name="y_1_%d" % i) for i in range(RING)]
+        cmp1_ring = [keep.tile([P, max(CHUNKS)], F32, name="cmp1_%d" % i) for i in range(RING)]
+        z_1_ring = [keep.tile([P, PACK, max(CHUNKS)], F32, name="z_1_%d" % i) for i in range(2)]
+
+        def gather_z_1(c, t):
+            cols = slice(starts[c] // 16, (starts[c] + CHUNKS[c]) // 16)
+            nc.scalar.activation(z_1[c][:, t, :], z_unit[t][:].indirect(dp1_sb[:, cols]), COPY)
+
+        def gather(c):
+            r0, n = starts[c], CHUNKS[c]
             cols = slice(r0 // 16, (r0 + n) // 16)
-            cfl = keep.tile([P, PACK, n], F32, name="cfl%d" % c)
-            z_1 = keep.tile([P, PACK, n], F32, name="z_1_%d" % c)
+            cfl[c] = keep.tile([P, PACK, n], F32, name="cfl%d" % c)
+            z_1[c] = z_1_ring[c % 2][:, :, 0:n]
             cmp1 = []
             for t in range(PACK + 1):
                 if t < PACK:
                     if c == 0:
                         project(t)
-                    y_1 = keep.tile([P, n], F32, name="y_1_%d_%d" % (c, t))
-                    prod = keep.tile([P, n], F32, name="cmp1_%d_%d" % (c, t))
-                    nc.scalar.activation(y_1[:], y[t][:].indirect(dp1_sb[:, cols]), COPY)
-                    nc.vector.tensor_tensor(prod[:], y[t][:].indirect(dp2_sb[:, cols]), y_1[:], MULT)
-                    nc.scalar.activation(z_1[:, t, :], z_unit[t][:].indirect(dp1_sb[:, cols]), COPY)
+                    y_1 = y_1_ring[(PACK * c + t) % RING][:, 0:n]
+                    prod = cmp1_ring[(PACK * c + t) % RING][:, 0:n]
+                    nc.scalar.activation(y_1, y[t][:].indirect(dp1_sb[:, cols]), COPY)
+                    nc.vector.tensor_tensor(prod, y[t][:].indirect(dp2_sb[:, cols]), y_1, MULT)
                     cmp1.append(prod)
                 if t > 0:
+                    if c > 0:
+                        gather_z_1(c - 1, t - 1)
                     nc.vector.tensor_tensor(
-                        cfl[:, t - 1, :], z_neg[t - 1][:].indirect(pk_sb[:, cols]), cmp1[t - 1][:], ADD
+                        cfl[c][:, t - 1, :], z_neg[t - 1][:].indirect(pk_sb[:, cols]), cmp1[t - 1], ADD
                     )
-            if c == 0:
-                deal_words(nc, raw_words[0], w_words[2])
-                deal_scales(nc, raw_scales[0], w_scales[2])
 
+        def multiply(c):
+            n = CHUNKS[c]
             hid = keep.tile([P, n * PACK], BF16, name="hid%d" % c, align_bytes=64)
             nc.vector.tensor_tensor(
                 hid[:].rearrange("p (j i t) -> p j t i", i=2, t=PACK),
-                cfl[:].rearrange("p t (j i) -> p j t i", i=2),
-                z_1[:].rearrange("p t (j i) -> p j t i", i=2),
+                cfl[c][:].rearrange("p t (j i) -> p j t i", i=2),
+                z_1[c].rearrange("p t (j i) -> p j t i", i=2),
                 MULT,
             )
             hid_codes = keep.tile([P, n], U32, name="hid_codes%d" % c, align_bytes=64)
             hid_plane = keep.tile([P, n], U8, name="hid_plane%d" % c, align_bytes=64)
             nc.vector.quantize_mx(out=hid_codes[:].bitcast(FP8X4), scales=hid_plane[:], in_=hid[:])
-
-            result = keep.tile([P, PACK, n], F32, name="result%d" % c)
-            rounded = keep.tile([P, n * PACK], BF16, name="rounded%d" % c, align_bytes=64)
+            banks[c] = []
             for s0 in range(0, n, SUB):
                 acc = last.tile([P, PACK, SUB], F32, name="acc")
                 for t in range(PACK):
@@ -175,11 +188,25 @@ def tile_picked_yresolv_cfl_po_kernel(
                         rhs_scale=hid_plane[:, s0 : s0 + SUB],
                         start=True, stop=True,
                     )
-                nc.scalar.copy(
-                    rounded[:, PACK * s0 : PACK * (s0 + SUB)].rearrange("p (j i t) -> p j t i", i=2, t=PACK),
-                    acc[:].rearrange("p t (j i) -> p j t i", i=2),
-                )
+                banks[c].append(acc)
+
+        def hand_out(c):
+            r0, n = starts[c], CHUNKS[c]
+            result = keep.tile([P, PACK, n], F32, name="result%d" % c)
+            rounded = keep.tile([P, n * PACK], BF16, name="rounded%d" % c, align_bytes=64)
+            for j, acc in enumerate(banks[c]):
+                s0 = j * SUB
                 nc.scalar.copy(result[:, :, s0 : s0 + SUB], acc[:])
+                if c < ROUNDED_FROM_PSUM:
+                    nc.scalar.copy(
+                        rounded[:, PACK * s0 : PACK * (s0 + SUB)].rearrange("p (j i t) -> p j t i", i=2, t=PACK),
+                        acc[:].rearrange("p t (j i) -> p j t i", i=2),
+                    )
+            if c >= ROUNDED_FROM_PSUM:
+                nc.vector.tensor_copy(
+                    rounded[:].rearrange("p (j i t) -> p j t i", i=4, t=PACK),
+                    result[:].rearrange("p t (j i) -> p j t i", i=4),
+                )
             nc.vector.quantize_mx(
                 out=out_codes[:, r0 : r0 + n].bitcast(FP8X4),
                 scales=out_plane[:, r0 : r0 + n],
@@ -190,7 +217,20 @@ def tile_picked_yresolv_cfl_po_kernel(
                 out=out_words[:, PACK * r0 : PACK * (r0 + n)].bitcast(I32),
                 in_=out_codes[:, r0 : r0 + n].bitcast(I32),
             )
-            r0 = r0 + n
+
+        gather(0)
+        deal_scales(nc, raw_scales[0], w_scales[2])
+        final = len(CHUNKS) - 1
+        for c in range(1, final + 1):
+            gather(c)
+            if c > 1:
+                hand_out(c - 2)
+            multiply(c - 1)
+        for t in range(PACK):
+            gather_z_1(final, t)
+        multiply(final)
+        hand_out(final - 1)
+        hand_out(final)
 
         for q in range(4):
             queue = nc.sync if q % 2 == 0 else nc.scalar

@@ -21,7 +21,7 @@ FLOPS = 2 * 512 * 512 * (S + S + U)
 CHUNKS = (256, 384, 256, 128)
 SUB = 128
 RING = 3
-ROUNDED_FROM_PSUM = 2
+ROUNDED_FROM_PSUM = 0
 
 
 def load_scale_rows(queues, plane, rows):
@@ -64,7 +64,7 @@ def tile_picked_yresolv_cfl_po_kernel(
         table_scales = keep.tile([P, T], U8, name="table_scales", align_bytes=64)
         raw_words = [keep.tile([P, 2 * S], U8, name="raw_words%d" % i) for i in range(3)]
         raw_scales = [keep.tile([P, S], U8, name="raw_scales%d" % i) for i in range(2)]
-        w_words = [keep.tile([P, 2 * S], U8, name="w_words%d" % i, align_bytes=64) for i in range(3)]
+        w_words = [keep.tile([P, 2 * S], U8, name="w_words%d" % i, align_bytes=64) for i in range(2)]
         w3_plane = keep.tile([P, S], U8, name="w3_plane", align_bytes=64)
         unit_sb = keep.tile([P, PACK], F32, name="unit_sb")
 
@@ -81,11 +81,11 @@ def tile_picked_yresolv_cfl_po_kernel(
             in_=x_words[0].rearrange("p n t -> p (n t)").bitcast(I32),
         )
         load_scale_rows([nc.sync] * 4, raw_scales[0], w1_scales)
-        nc.gpsimd.dma_start(out=raw_words[2][:].bitcast(I32), in_=w3_words[0].bitcast(I32))
-        load_scale_rows([nc.gpsimd] + [nc.sync] * 3, raw_scales[1], w2_scales)
-        nc.gpsimd.dma_start(out=unit_sb[:], in_=unit.rearrange("(p t) o -> p (t o)", t=PACK))
         nc.sync.dma_start(dp1_sb[:], dp1)
+        nc.sync.dma_start(out=raw_words[2][:].bitcast(I32), in_=w3_words[0].bitcast(I32))
+        load_scale_rows([nc.sync] * 4, raw_scales[1], w2_scales)
         nc.sync.dma_start(dp2_sb[:], dp2)
+        nc.sync.dma_start(out=unit_sb[:], in_=unit.rearrange("(p t) o -> p (t o)", t=PACK))
         nc.sync.dma_start(pk_sb[:], pk)
 
         x_codes = keep.tile([P, S], U32, name="x_codes", align_bytes=64)
@@ -93,11 +93,12 @@ def tile_picked_yresolv_cfl_po_kernel(
         deal_words(nc, raw_words[0], w_words[0][:])
         nc.vector.tensor_copy(x_plane[:], table_scales[:].indirect(offs_sb[:]))
         deal_words(nc, raw_words[1], w_words[1][:])
-        deal_words(nc, raw_words[2], w_words[2][:])
         nc.vector.tensor_copy(x_codes[:], table_words[:].indirect(offs_sb[:]))
-        late = keep.tile([P, 2 * S], U8, name="late", tag="table", align_bytes=64)
+        late = keep.tile([P, 4 * S], U8, name="late", tag="table", align_bytes=64)
         w_scales = [late[:, 0:S], late[:, S : 2 * S], w3_plane[:]]
         deal_scales(nc, raw_scales[0], w_scales[0])
+        w_words.append(late[:, 2 * S : 4 * S])
+        deal_words(nc, raw_words[2], w_words[2])
         deal_scales(nc, raw_scales[1], w_scales[1])
         load_scale_rows([nc.sync] * 4, raw_scales[0], w3_scales)
 
@@ -111,22 +112,15 @@ def tile_picked_yresolv_cfl_po_kernel(
         z_neg = [keep.tile([P, S], F32, name="z_neg%d" % t) for t in range(PACK)]
         z_unit = [keep.tile([P, S], F32, name="z_unit%d" % t) for t in range(PACK)]
 
-        def project(t):
-            banks = []
-            for i in range(2):
-                bank = first.tile([P, S], F32, name="bank")
-                words, scales = stationary(i, t)
-                nc.tensor.matmul_mx(
-                    out=bank[:], lhsT=words, lhsT_scale=scales,
-                    rhs=x_codes[:].bitcast(FP8X4), rhs_scale=x_plane[:],
-                    start=True, stop=True,
-                )
-                banks.append(bank)
-            nc.scalar.activation(y[t][:], banks[0][:], COPY)
-            nc.scalar.mul(z_neg[t][:], banks[1][:], -1.0)
-            nc.vector.tensor_scalar(
-                z_unit[t][:], z_neg[t][:], unit_sb[:, t : t + 1], -1.0, MULT, MULT
+        def project(i, t):
+            bank = first.tile([P, S], F32, name="bank")
+            words, scales = stationary(i, t)
+            nc.tensor.matmul_mx(
+                out=bank[:], lhsT=words, lhsT_scale=scales,
+                rhs=x_codes[:].bitcast(FP8X4), rhs_scale=x_plane[:],
+                start=True, stop=True,
             )
+            return bank
 
         out_codes = keep.tile([P, U], U32, name="out_codes", align_bytes=64)
         out_plane = keep.tile([P, U], U8, name="out_plane", align_bytes=64)
@@ -150,20 +144,28 @@ def tile_picked_yresolv_cfl_po_kernel(
             z_1[c] = z_1_ring[c % 2][:, :, 0:n]
             cmp1 = []
             for t in range(PACK + 1):
+                if t == 2 and c > 1:
+                    hand_out(c - 2)
                 if t < PACK:
                     if c == 0:
-                        project(t)
+                        nc.scalar.activation(y[t][:], project(0, t)[:], COPY)
                     y_1 = y_1_ring[(PACK * c + t) % RING][:, 0:n]
                     prod = cmp1_ring[(PACK * c + t) % RING][:, 0:n]
                     nc.scalar.activation(y_1, y[t][:].indirect(dp1_sb[:, cols]), COPY)
                     nc.vector.tensor_tensor(prod, y[t][:].indirect(dp2_sb[:, cols]), y_1, MULT)
                     cmp1.append(prod)
                 if t > 0:
+                    if c == 0:
+                        nc.scalar.mul(z_neg[t - 1][:], project(1, t - 1)[:], -1.0)
                     if c > 0:
                         gather_z_1(c - 1, t - 1)
                     nc.vector.tensor_tensor(
                         cfl[c][:, t - 1, :], z_neg[t - 1][:].indirect(pk_sb[:, cols]), cmp1[t - 1], ADD
                     )
+                    if c == 0:
+                        nc.vector.tensor_scalar(
+                            z_unit[t - 1][:], z_neg[t - 1][:], unit_sb[:, t - 1 : t], -1.0, MULT, MULT
+                        )
 
         def multiply(c):
             n = CHUNKS[c]
@@ -223,8 +225,6 @@ def tile_picked_yresolv_cfl_po_kernel(
         final = len(CHUNKS) - 1
         for c in range(1, final + 1):
             gather(c)
-            if c > 1:
-                hand_out(c - 2)
             multiply(c - 1)
         for t in range(PACK):
             gather_z_1(final, t)

@@ -21,7 +21,7 @@ FLOPS = 2 * 512 * 512 * (S + S + U)
 CHUNKS = (256, 384, 256, 128)
 SUB = 128
 RING = 3
-ROUNDED_FROM_PSUM = 0
+ROUNDED_FROM_PSUM = 1
 
 
 def load_scale_rows(queues, plane, rows):
@@ -53,8 +53,7 @@ def tile_picked_yresolv_cfl_po_kernel(
     nc = tc.nc
     with ExitStack() as ctx:
         keep = ctx.enter_context(tc.tile_pool(name="keep", bufs=1))
-        first = ctx.enter_context(tc.psum_pool(name="first", bufs=4))
-        last = ctx.enter_context(tc.psum_pool(name="last", bufs=4))
+        psum = ctx.enter_context(tc.psum_pool(name="psum", bufs=8))
 
         offs_sb = keep.tile([P, S // 16], U16, name="offs_sb")
         pk_sb = keep.tile([P, U // 16], U16, name="pk_sb")
@@ -113,7 +112,7 @@ def tile_picked_yresolv_cfl_po_kernel(
         z_unit = [keep.tile([P, S], F32, name="z_unit%d" % t) for t in range(PACK)]
 
         def project(i, t):
-            bank = first.tile([P, S], F32, name="bank")
+            bank = psum.tile([P, S], F32, name="bank")
             words, scales = stationary(i, t)
             nc.tensor.matmul_mx(
                 out=bank[:], lhsT=words, lhsT_scale=scales,
@@ -129,6 +128,7 @@ def tile_picked_yresolv_cfl_po_kernel(
 
         starts = [sum(CHUNKS[:c]) for c in range(len(CHUNKS))]
         cfl, z_1, banks = {}, {}, {}
+        final = len(CHUNKS) - 1
         y_1_ring = [keep.tile([P, max(CHUNKS)], F32, name="y_1_%d" % i) for i in range(RING)]
         cmp1_ring = [keep.tile([P, max(CHUNKS)], F32, name="cmp1_%d" % i) for i in range(RING)]
         z_1_ring = [keep.tile([P, PACK, max(CHUNKS)], F32, name="z_1_%d" % i) for i in range(2)]
@@ -157,7 +157,9 @@ def tile_picked_yresolv_cfl_po_kernel(
                 if t > 0:
                     if c == 0:
                         nc.scalar.mul(z_neg[t - 1][:], project(1, t - 1)[:], -1.0)
-                    if c > 0:
+                    if c == final:
+                        gather_z_1(c, t - 1)
+                    elif c > 0:
                         gather_z_1(c - 1, t - 1)
                     nc.vector.tensor_tensor(
                         cfl[c][:, t - 1, :], z_neg[t - 1][:].indirect(pk_sb[:, cols]), cmp1[t - 1], ADD
@@ -181,7 +183,18 @@ def tile_picked_yresolv_cfl_po_kernel(
             nc.vector.quantize_mx(out=hid_codes[:].bitcast(FP8X4), scales=hid_plane[:], in_=hid[:])
             banks[c] = []
             for s0 in range(0, n, SUB):
-                acc = last.tile([P, PACK, SUB], F32, name="acc")
+                if c == final:
+                    halves = [psum.tile([P, 2, SUB], F32, name="half%d" % h, tag="bank") for h in range(2)]
+                    for t in range(PACK):
+                        words, scales = stationary(2, t)
+                        nc.tensor.matmul_mx(
+                            out=halves[t // 2][:, t % 2, :], lhsT=words, lhsT_scale=scales,
+                            rhs=hid_codes[:].bitcast(FP8X4), rhs_scale=hid_plane[:],
+                            start=True, stop=True,
+                        )
+                    banks[c] = halves
+                    continue
+                acc = psum.tile([P, PACK, SUB], F32, name="acc", tag="bank")
                 for t in range(PACK):
                     words, scales = stationary(2, t)
                     nc.tensor.matmul_mx(
@@ -198,6 +211,12 @@ def tile_picked_yresolv_cfl_po_kernel(
             rounded = keep.tile([P, n * PACK], BF16, name="rounded%d" % c, align_bytes=64)
             for j, acc in enumerate(banks[c]):
                 s0 = j * SUB
+                if c == final:
+                    if j == 0:
+                        nc.scalar.copy(result[:, 0:2, :], acc[:])
+                    else:
+                        nc.vector.tensor_copy(result[:, 2:4, :], acc[:])
+                    continue
                 nc.scalar.copy(result[:, :, s0 : s0 + SUB], acc[:])
                 if c < ROUNDED_FROM_PSUM:
                     nc.scalar.copy(
@@ -222,12 +241,13 @@ def tile_picked_yresolv_cfl_po_kernel(
 
         gather(0)
         deal_scales(nc, raw_scales[0], w_scales[2])
-        final = len(CHUNKS) - 1
-        for c in range(1, final + 1):
+        for c in range(1, final):
             gather(c)
             multiply(c - 1)
         for t in range(PACK):
-            gather_z_1(final, t)
+            gather_z_1(final - 1, t)
+        multiply(final - 1)
+        gather(final)
         multiply(final)
         hand_out(final - 1)
         hand_out(final)

from contextlib import ExitStack

import concourse.mybir as mybir

F32 = mybir.dt.float32
BF16 = mybir.dt.bfloat16
I32 = mybir.dt.int32
U32 = mybir.dt.uint32
U16 = mybir.dt.uint16
U8 = mybir.dt.uint8
FP8X4 = mybir.dt.float8_e4m3fn_x4
FP4X4 = mybir.dt.float4_e2m1fn_x4
MULT = mybir.AluOpType.mult
ADD = mybir.AluOpType.add
COPY = mybir.ActivationFunctionType.Copy

P = 128
PACK = 4
T, S, U = 2048, 512, 1024
FLOPS = 2 * 512 * 512 * (S + S + U)
CHUNKS = (256, 384, 256, 128)
SUB = 128
RING = 3
ROUNDED_FROM_PSUM = 1


def load_scale_rows(queues, plane, rows):
    for q in range(4):
        queues[q].dma_start(
            out=plane[32 * q : 32 * q + 4, :].bitcast(I32),
            in_=rows[0, 4 * q : 4 * q + 4, :].bitcast(I32),
        )


def deal_words(nc, raw_words, words):
    nc.vector.tensor_copy(
        out=words.rearrange("p (t m b) -> p t m b", t=PACK, b=2),
        in_=raw_words[:].rearrange("p (m t b) -> p t m b", t=PACK, b=2),
    )


def deal_scales(nc, raw_scales, scales):
    nc.vector.tensor_copy(
        out=scales.rearrange("p (t m) -> p t m", t=PACK),
        in_=raw_scales[:].rearrange("p (m t) -> p t m", t=PACK),
    )


def tile_picked_yresolv_cfl_po_kernel(
    tc, x_words, x_scales, w1_words, w1_scales, w2_words, w2_scales, unit,
    w3_words, w3_scales, offs, pk, dp1, dp2, out_0, out_1, out_2,
):
    nc = tc.nc
    with ExitStack() as ctx:
        keep = ctx.enter_context(tc.tile_pool(name="keep", bufs=1))
        psum = ctx.enter_context(tc.psum_pool(name="psum", bufs=8))

        offs_sb = keep.tile([P, S // 16], U16, name="offs_sb")
        pk_sb = keep.tile([P, U // 16], U16, name="pk_sb")
        dp1_sb = keep.tile([P, U // 16], U16, name="dp1_sb")
        dp2_sb = keep.tile([P, U // 16], U16, name="dp2_sb")
        table_words = keep.tile([P, T], U32, name="table_words", tag="table", align_bytes=64)
        table_scales = keep.tile([P, T], U8, name="table_scales", align_bytes=64)
        raw_words = [keep.tile([P, 2 * S], U8, name="raw_words%d" % i) for i in range(3)]
        raw_scales = [keep.tile([P, S], U8, name="raw_scales%d" % i) for i in range(2)]
        w_words = [keep.tile([P, 2 * S], U8, name="w_words%d" % i, align_bytes=64) for i in range(2)]
        w3_plane = keep.tile([P, S], U8, name="w3_plane", align_bytes=64)
        unit_sb = keep.tile([P, PACK], F32, name="unit_sb")

        nc.vector.memset(table_scales[:].bitcast(I32), 0)
        for i in range(2):
            nc.vector.memset(raw_scales[i][:].bitcast(I32), 0)

        nc.sync.dma_start(out=raw_words[0][:].bitcast(I32), in_=w1_words[0].bitcast(I32))
        nc.sync.dma_start(offs_sb[:], offs)
        load_scale_rows([nc.sync] * 4, table_scales, x_scales)
        nc.sync.dma_start(out=raw_words[1][:].bitcast(I32), in_=w2_words[0].bitcast(I32))
        nc.sync.dma_start(
            out=table_words[:].bitcast(I32),
            in_=x_words[0].rearrange("p n t -> p (n t)").bitcast(I32),
        )
        load_scale_rows([nc.sync] * 4, raw_scales[0], w1_scales)
        nc.sync.dma_start(dp1_sb[:], dp1)
        nc.sync.dma_start(out=raw_words[2][:].bitcast(I32), in_=w3_words[0].bitcast(I32))
        load_scale_rows([nc.sync] * 4, raw_scales[1], w2_scales)
        nc.sync.dma_start(dp2_sb[:], dp2)
        nc.sync.dma_start(out=unit_sb[:], in_=unit.rearrange("(p t) o -> p (t o)", t=PACK))
        nc.sync.dma_start(pk_sb[:], pk)

        x_codes = keep.tile([P, S], U32, name="x_codes", align_bytes=64)
        x_plane = keep.tile([P, S], U8, name="x_plane", align_bytes=64)
        deal_words(nc, raw_words[0], w_words[0][:])
        nc.vector.tensor_copy(x_plane[:], table_scales[:].indirect(offs_sb[:]))
        deal_words(nc, raw_words[1], w_words[1][:])
        nc.vector.tensor_copy(x_codes[:], table_words[:].indirect(offs_sb[:]))
        late = keep.tile([P, 4 * S], U8, name="late", tag="table", align_bytes=64)
        w_scales = [late[:, 0:S], late[:, S : 2 * S], w3_plane[:]]
        deal_scales(nc, raw_scales[0], w_scales[0])
        w_words.append(late[:, 2 * S : 4 * S])
        deal_words(nc, raw_words[2], w_words[2])
        deal_scales(nc, raw_scales[1], w_scales[1])
        load_scale_rows([nc.sync] * 4, raw_scales[0], w3_scales)

        def stationary(i, t):
            return (
                w_words[i][:, 2 * P * t : 2 * P * (t + 1)].bitcast(FP4X4),
                w_scales[i][:, P * t : P * (t + 1)],
            )

        y = [keep.tile([P, S], F32, name="y%d" % t) for t in range(PACK)]
        z_neg = [keep.tile([P, S], F32, name="z_neg%d" % t) for t in range(PACK)]
        z_unit = [keep.tile([P, S], F32, name="z_unit%d" % t) for t in range(PACK)]

        def project(i, t):
            bank = psum.tile([P, S], F32, name="bank")
            words, scales = stationary(i, t)
            nc.tensor.matmul_mx(
                out=bank[:], lhsT=words, lhsT_scale=scales,
                rhs=x_codes[:].bitcast(FP8X4), rhs_scale=x_plane[:],
                start=True, stop=True,
            )
            return bank

        out_codes = keep.tile([P, U], U32, name="out_codes", align_bytes=64)
        out_plane = keep.tile([P, U], U8, name="out_plane", align_bytes=64)
        out_rows = out_0.rearrange("(p t) r -> p t r", t=PACK)
        out_words = out_1[0].rearrange("p n t -> p (n t)")

        starts = [sum(CHUNKS[:c]) for c in range(len(CHUNKS))]
        cfl, z_1, banks = {}, {}, {}
        final = len(CHUNKS) - 1
        y_1_ring = [keep.tile([P, max(CHUNKS)], F32, name="y_1_%d" % i) for i in range(RING)]
        cmp1_ring = [keep.tile([P, max(CHUNKS)], F32, name="cmp1_%d" % i) for i in range(RING)]
        z_1_ring = [keep.tile([P, PACK, max(CHUNKS)], F32, name="z_1_%d" % i) for i in range(2)]

        def gather_z_1(c, t):
            cols = slice(starts[c] // 16, (starts[c] + CHUNKS[c]) // 16)
            nc.scalar.activation(z_1[c][:, t, :], z_unit[t][:].indirect(dp1_sb[:, cols]), COPY)

        def gather(c):
            r0, n = starts[c], CHUNKS[c]
            cols = slice(r0 // 16, (r0 + n) // 16)
            cfl[c] = keep.tile([P, PACK, n], F32, name="cfl%d" % c)
            z_1[c] = z_1_ring[c % 2][:, :, 0:n]
            cmp1 = []
            for t in range(PACK + 1):
                if t == 2 and c > 1:
                    hand_out(c - 2)
                if t < PACK:
                    if c == 0:
                        nc.scalar.activation(y[t][:], project(0, t)[:], COPY)
                    y_1 = y_1_ring[(PACK * c + t) % RING][:, 0:n]
                    prod = cmp1_ring[(PACK * c + t) % RING][:, 0:n]
                    nc.scalar.activation(y_1, y[t][:].indirect(dp1_sb[:, cols]), COPY)
                    nc.vector.tensor_tensor(prod, y[t][:].indirect(dp2_sb[:, cols]), y_1, MULT)
                    cmp1.append(prod)
                if t > 0:
                    if c == 0:
                        nc.scalar.mul(z_neg[t - 1][:], project(1, t - 1)[:], -1.0)
                    if c == final:
                        gather_z_1(c, t - 1)
                    elif c > 0:
                        gather_z_1(c - 1, t - 1)
                    nc.vector.tensor_tensor(
                        cfl[c][:, t - 1, :], z_neg[t - 1][:].indirect(pk_sb[:, cols]), cmp1[t - 1], ADD
                    )
                    if c == 0:
                        nc.vector.tensor_scalar(
                            z_unit[t - 1][:], z_neg[t - 1][:], unit_sb[:, t - 1 : t], -1.0, MULT, MULT
                        )

        def multiply(c):
            n = CHUNKS[c]
            hid = keep.tile([P, n * PACK], BF16, name="hid%d" % c, align_bytes=64)
            nc.vector.tensor_tensor(
                hid[:].rearrange("p (j i t) -> p j t i", i=2, t=PACK),
                cfl[c][:].rearrange("p t (j i) -> p j t i", i=2),
                z_1[c].rearrange("p t (j i) -> p j t i", i=2),
                MULT,
            )
            hid_codes = keep.tile([P, n], U32, name="hid_codes%d" % c, align_bytes=64)
            hid_plane = keep.tile([P, n], U8, name="hid_plane%d" % c, align_bytes=64)
            nc.vector.quantize_mx(out=hid_codes[:].bitcast(FP8X4), scales=hid_plane[:], in_=hid[:])
            banks[c] = []
            for s0 in range(0, n, SUB):
                if c == final:
                    halves = [psum.tile([P, 2, SUB], F32, name="half%d" % h, tag="bank") for h in range(2)]
                    for t in range(PACK):
                        words, scales = stationary(2, t)
                        nc.tensor.matmul_mx(
                            out=halves[t // 2][:, t % 2, :], lhsT=words, lhsT_scale=scales,
                            rhs=hid_codes[:].bitcast(FP8X4), rhs_scale=hid_plane[:],
                            start=True, stop=True,
                        )
                    banks[c] = halves
                    continue
                acc = psum.tile([P, PACK, SUB], F32, name="acc", tag="bank")
                for t in range(PACK):
                    words, scales = stationary(2, t)
                    nc.tensor.matmul_mx(
                        out=acc[:, t, :], lhsT=words, lhsT_scale=scales,
                        rhs=hid_codes[:, s0 : s0 + SUB].bitcast(FP8X4),
                        rhs_scale=hid_plane[:, s0 : s0 + SUB],
                        start=True, stop=True,
                    )
                banks[c].append(acc)

        def hand_out(c):
            r0, n = starts[c], CHUNKS[c]
            result = keep.tile([P, PACK, n], F32, name="result%d" % c)
            rounded = keep.tile([P, n * PACK], BF16, name="rounded%d" % c, align_bytes=64)
            for j, acc in enumerate(banks[c]):
                s0 = j * SUB
                if c == final:
                    if j == 0:
                        nc.scalar.copy(result[:, 0:2, :], acc[:])
                    else:
                        nc.vector.tensor_copy(result[:, 2:4, :], acc[:])
                    continue
                nc.scalar.copy(result[:, :, s0 : s0 + SUB], acc[:])
                if c < ROUNDED_FROM_PSUM:
                    nc.scalar.copy(
                        rounded[:, PACK * s0 : PACK * (s0 + SUB)].rearrange("p (j i t) -> p j t i", i=2, t=PACK),
                        acc[:].rearrange("p t (j i) -> p j t i", i=2),
                    )
            if c >= ROUNDED_FROM_PSUM:
                nc.vector.tensor_copy(
                    rounded[:].rearrange("p (j i t) -> p j t i", i=4, t=PACK),
                    result[:].rearrange("p t (j i) -> p j t i", i=4),
                )
            nc.vector.quantize_mx(
                out=out_codes[:, r0 : r0 + n].bitcast(FP8X4),
                scales=out_plane[:, r0 : r0 + n],
                in_=rounded[:],
            )
            nc.sync.dma_start(out=out_rows[:, :, r0 : r0 + n], in_=result[:])
            nc.sync.dma_start(
                out=out_words[:, PACK * r0 : PACK * (r0 + n)].bitcast(I32),
                in_=out_codes[:, r0 : r0 + n].bitcast(I32),
            )

        gather(0)
        deal_scales(nc, raw_scales[0], w_scales[2])
        for c in range(1, final):
            gather(c)
            multiply(c - 1)
        for t in range(PACK):
            gather_z_1(final - 1, t)
        multiply(final - 1)
        gather(final)
        multiply(final)
        hand_out(final - 1)
        hand_out(final)

        for q in range(4):
            queue = nc.sync if q % 2 == 0 else nc.scalar
            queue.dma_start(
                out=out_2[0, 4 * q : 4 * q + 4, :].bitcast(I32),
                in_=out_plane[32 * q : 32 * q + 4, :].bitcast(I32),
            )
